import numpy as np
import ml_dtypes


def mxq(x, axis, fmt="e4m3"):
    dtype, down = {"e4m3": (ml_dtypes.float8_e4m3fn, 7), "e5m2": (ml_dtypes.float8_e5m2, 14)}[fmt]
    v = np.moveaxis(np.asarray(x, np.float32).astype(ml_dtypes.bfloat16).astype(np.float64), axis, -1)
    blocks = v.reshape(v.shape[:-1] + (-1, 32))
    amax = np.abs(blocks).max(-1, keepdims=True)
    byte = np.maximum(np.where(amax > 0, np.frexp(amax)[1] - 1 + 127, 0) - down, 1)
    scale = np.exp2(byte - 127.0)
    codes = (blocks / scale).astype(np.float32).astype(dtype).astype(np.float64)
    return np.moveaxis((codes * scale).reshape(v.shape), -1, axis)


WIDE = False


def mx_kscale(k):
    if not WIDE:
        return np.ones(k)
    levels = np.array([10, -10, 5, -5, 0])
    if k % 512:
        return np.exp2(np.random.permutation(np.resize(levels, k // 32))).repeat(32)
    a = np.empty((k // 512, 16))
    for p in range(k // 512):
        a[p, :8] = np.random.permutation(np.resize(levels, 8))
        for g in range(8):
            far = levels[np.abs(levels - a[p, g]) >= 10]
            a[p, g + 8] = far[np.random.randint(len(far))]
    return np.exp2(a.ravel()).repeat(32)


def f64(x):
    return np.asarray(x).astype(np.float64)


def striped(idx):
    return np.tile(idx.reshape(-1, 16).T, (8, 1)).astype(np.uint16)


def unstriped(offs):
    return offs[:16].T.reshape(-1).astype(np.int64)


def pack_weight(w):
    k, n = w.shape
    w = f64(np.asarray(w, np.float32).astype(ml_dtypes.bfloat16)).reshape(k // 32, 32, n)
    amax = np.abs(w).max(1)
    byte = np.clip(np.where(amax > 0, np.frexp(amax)[1] - 1 + 127 - 7, 1), 1, 254)
    scaled = (w * np.exp2(127.0 - byte)[:, None, :]).reshape(k, n).astype(np.float32)
    words = np.ascontiguousarray(scaled.reshape(k // 512, 128, 4, n).transpose(0, 1, 3, 2)).astype(ml_dtypes.float8_e4m3fn).view(np.uint8)
    return words, np.ascontiguousarray(byte.astype(np.uint8).reshape(k // 512, 16, n))


def unpack_weight(words, scales):
    g, p, n, _ = words.shape
    vals = np.ascontiguousarray(words).view(ml_dtypes.float8_e4m3fn).astype(np.float64) * np.repeat(np.exp2(scales.astype(np.float64) - 127.0), 8, axis=1)[..., None]
    return vals.transpose(0, 1, 3, 2).reshape(g * 512, n)


K, T, S, N, H = 512, 1024, 512, 128, 512


def setup_inputs():
    n = np.random.standard_normal
    s = mx_kscale(K)[:, None]
    u = mx_kscale(H)
    packed_xT = pack_weight(n((K, T)) * s)
    return {
        "x_words": packed_xT[0],
        "x_scales": packed_xT[1],
        "w1": (n((K, H)) / np.sqrt(K) / s).astype(np.float32),
        "w2": (n((K, H)) / np.sqrt(K) / s).astype(np.float32),
        "sig": (np.random.uniform(0.3, 1.2, (H, S))).astype(np.float32),
        "unit": (np.random.uniform(0.6, 1.4, (H, 1)) * u[:, None]).astype(np.float32),
        "w3": (n((H, N)) / np.sqrt(H) / u[:, None]).astype(np.float32),
        "offs": striped(np.random.permutation(T)[:S]),
        "reg": striped(np.random.permutation(S)),
    }


def reference(x_words, x_scales, w1, w2, sig, unit, w3, offs, reg):
    xq = unpack_weight(x_words, x_scales)[:, unstriped(offs)]
    sr = mxq(f64(w1), 0, "e4m3").T @ xq
    sf = mxq(f64(w2), 0, "e4m3").T @ xq
    drc = (sr - sf) / f64(sig)
    ad = np.abs(drc)
    nrm = ad.mean(axis=1, keepdims=True)
    gd = drc / (nrm + 0.2)
    fr = sf[:, unstriped(reg)]
    rg = fr - sf
    hid = f64(unit) * (gd + 0.6 * np.tanh(rg))
    return mxq(f64(w3), 0, "e4m3").T @ mxq(hid, 0, "e4m3")

@@ -1,0 +1,397 @@
+from contextlib import ExitStack
+
+import concourse.mybir as mybir
+from concourse.masks import make_identity
+
+K, T, S, N, H = 512, 1024, 512, 128, 512
+FLOPS = 2 * K * H * S * 2 + 2 * H * N * S
+
+F32 = mybir.dt.float32
+BF16 = mybir.dt.bfloat16
+I32 = mybir.dt.int32
+U32 = mybir.dt.uint32
+U16 = mybir.dt.uint16
+U8 = mybir.dt.uint8
+FP8X4 = mybir.dt.float8_e4m3fn_x4
+ALU = mybir.AluOpType
+ACT = mybir.ActivationFunctionType
+
+P = 128
+PACK = 4
+HALF = 256
+
+
+def tile_picked_ydmddi_reg_p_kernel(
+    tc, x_words, x_scales, w1, w2, sig, unit, w3, offs, reg, out
+):
+    nc = tc.nc
+    with ExitStack() as ctx:
+        keep = ctx.enter_context(tc.tile_pool(name="keep", bufs=1))
+        psum = ctx.enter_context(tc.psum_pool(name="psum", bufs=1))
+
+        def sb(name, shape, dtype):
+            return keep.tile(shape, dtype, name=name, align_bytes=64)
+
+        offs_sb = sb("offs_sb", [P, S // 16], U16)
+        reg_sb = sb("reg_sb", [P, S // 16], U16)
+        xw = sb("xw", [P, T], I32)
+        xs = sb("xs", [P, T], U8)
+        sig_sb = [sb("sig%d" % t, [P, S], F32) for t in range(PACK)]
+        w1_raw = [sb("w1raw%d" % h, [P, PACK, HALF], F32) for h in range(2)]
+        w2_raw = [sb("w2raw%d" % h, [P, PACK, HALF], F32) for h in range(2)]
+        w3_raw = sb("w3raw", [P, PACK, N], F32)
+        unit_sb = sb("unit_sb", [P, PACK], F32)
+
+        sig_v = sig.rearrange("(p t) j -> p t j", t=PACK)
+        w1_v = w1.rearrange("(p j) c -> p j c", j=PACK)
+        w2_v = w2.rearrange("(p j) c -> p j c", j=PACK)
+
+        nc.vector.memset(xs[:].bitcast(I32), 0)
+        for q in range(4):
+            nc.scalar.dma_start(
+                out=xs[32 * q : 32 * q + 4, :].bitcast(I32),
+                in_=x_scales[0, 4 * q : 4 * q + 4, :].bitcast(I32),
+            )
+
+        def load_sig(t):
+            nc.sync.dma_start(out=sig_sb[t][:], in_=sig_v[:, t, :])
+
+        def load_w(raw, view, h):
+            nc.sync.dma_start(out=raw[h][:], in_=view[:, :, h * HALF : (h + 1) * HALF])
+
+        def load_x():
+            nc.sync.dma_start(out=xw[:], in_=x_words[0].rearrange("p n t -> p (n t)").bitcast(I32))
+
+        load_sig(0)
+        nc.sync.dma_start(offs_sb[:], offs)
+        load_sig(1)
+        load_x()
+        load_sig(2)
+        load_sig(3)
+        load_w(w2_raw, w2_v, 0)
+        load_w(w2_raw, w2_v, 1)
+        nc.sync.dma_start(out=unit_sb[:], in_=unit.rearrange("(p t) o -> p (t o)", t=PACK))
+        nc.sync.dma_start(reg_sb[:], reg)
+        load_w(w1_raw, w1_v, 0)
+        load_w(w1_raw, w1_v, 1)
+        nc.sync.dma_start(out=w3_raw[:], in_=w3.rearrange("(p j) n -> p j n", j=PACK))
+
+        ident = sb("ident", [P, P], F32)
+        make_identity(nc, ident[:])
+
+        root = [sb("root%d" % t, [P, S], F32) for t in range(PACK)]
+        inv = [sb("inv%d" % t, [P, S], F32) for t in range(PACK)]
+        sgn = [sb("sgn%d" % t, [P, S], F32) for t in range(PACK)]
+
+        def inv_root(t):
+            nc.scalar.activation(out=root[t][:], in_=sig_sb[t][:], func=ACT.Abs_reciprocal_sqrt)
+
+        def inv_square(t):
+            nc.scalar.activation(out=inv[t][:], in_=root[t][:], func=ACT.Square)
+
+        def half_sign(t):
+            nc.vector.tensor_scalar(sgn[t][:], sig_sb[t][:], 0.0, 0.5, ALU.is_ge, ALU.subtract)
+
+        xg = sb("xg", [P, S], U32)
+        xsg = sb("xsg", [P, S], U8)
+
+        def gather_x():
+            nc.vector.tensor_copy(xg[:], xw[:].bitcast(U32).indirect(offs_sb[:]))
+            nc.vector.tensor_copy(xsg[:], xs[:].indirect(offs_sb[:]))
+
+        wb = {1: sb("w1b", [P, PACK, P, PACK], BF16), 2: sb("w2b", [P, PACK, P, PACK], BF16)}
+        wraw = {1: w1_raw, 2: w2_raw}
+        wc = {1: sb("w1c", [P, H], U32), 2: sb("w2c", [P, H], U32)}
+        wsc = {1: sb("w1s", [P, H], U8), 2: sb("w2s", [P, H], U8)}
+
+        def cast_w(w, h, eng, t0=0, t1=PACK):
+            dst = wb[w][:, t0:t1, 64 * h : 64 * (h + 1), :].rearrange("p t m j -> p m j t")
+            src = wraw[w][h][:].rearrange("p j (m t) -> p m j t", t=PACK)[:, :, :, t0:t1]
+            if w == 1 and eng == "v":
+                nc.vector.tensor_scalar(dst, src, -1.0, None, ALU.mult)
+            elif w == 1:
+                nc.scalar.activation(out=dst, in_=src, func=ACT.Copy, scale=-1.0)
+            elif eng == "v":
+                nc.vector.tensor_copy(out=dst, in_=src)
+            else:
+                nc.scalar.copy(out=dst, in_=src)
+
+        def quant_w(w, t0, t1):
+            nc.vector.quantize_mx(
+                out=wc[w][:, t0 * P : t1 * P].bitcast(FP8X4),
+                scales=wsc[w][:, t0 * P : t1 * P],
+                in_=wb[w][:, t0:t1].rearrange("p t m j -> p (t m j)"),
+            )
+
+        w3b = sb("w3b", [P, N, PACK], BF16)
+        w3c = sb("w3c", [P, N], U32)
+        w3s = sb("w3s", [P, N], U8)
+
+        def cast_w3():
+            nc.vector.tensor_copy(
+                out=w3b[:].rearrange("p (c i) j -> p c j i", i=4),
+                in_=w3_raw[:].rearrange("p j (c i) -> p c j i", i=4),
+            )
+
+        def quant_w3():
+            nc.vector.quantize_mx(
+                out=w3c[:].bitcast(FP8X4), scales=w3s[:], in_=w3b[:].rearrange("p n j -> p (n j)")
+            )
+
+        def product(w, t, bank, start=True, stop=True):
+            cols = slice(t * P, (t + 1) * P)
+            nc.tensor.matmul_mx(
+                out=bank[:],
+                lhsT=wc[w][:, cols].bitcast(FP8X4),
+                lhsT_scale=wsc[w][:, cols],
+                rhs=xg[:].bitcast(FP8X4),
+                rhs_scale=xsg[:],
+                start=start,
+                stop=stop,
+            )
+
+        sf_sb = [sb("sf%d" % t, [P, S], F32) for t in range(PACK)]
+        nfr = [sb("nfr%d" % t, [P, S], F32) for t in range(PACK)]
+        th_t = [sb("tht%d" % t, [P, PACK, P], F32) for t in range(PACK)]
+        dif = [sb("dif%d" % t, [P, S], F32) for t in range(PACK)]
+        z = [sb("z%d" % t, [P, S], F32) for t in range(PACK)]
+        e = [sb("e%d" % t, [P, S], F32) for t in range(PACK)]
+        absz = sb("absz", [P, S], F32)
+        sums = [sb("sum%d" % t, [P, 1], F32) for t in range(PACK)]
+        den = [sb("den%d" % t, [P, 1], F32) for t in range(PACK)]
+        scaled_unit = sb("scaled_unit", [P, PACK], F32)
+        per_unit = sb("per_unit", [P, PACK], F32)
+        c1 = [sb("c1_%d" % t, [P, 1], F32) for t in range(PACK)]
+        c2 = sb("c2", [P, PACK], F32)
+        hid_p = [sb("hidp%d" % h, [P, PACK, HALF], BF16) for h in range(2)]
+        hid_i = [sb("hidi%d" % h, [P, HALF, PACK], BF16) for h in range(2)]
+        hc = [sb("hc%d" % h, [P, HALF], U32) for h in range(2)]
+        hs = [sb("hs%d" % h, [P, HALF], U8) for h in range(2)]
+        res = [sb("res%d" % h, [P, HALF], F32) for h in range(2)]
+        bank = {}
+        place = {"sf0":0,"sf1":1,"sf2":2,"sf3":3,"sr0":4,"sr1":5,"sr2":6,"sr3":7,"tt00":0,"tt01":1,"tt10":2,"tt11":3,"th00":4,"th01":5,"th10":6,"th11":7,"out0":0,"out1":1}
+
+        def take(key, shape):
+            tag = "bank%d" % place[key]
+            return psum.tile(shape, F32, name=tag, tag=tag, bufs=1)
+
+        def sf_mm(t):
+            bank["sf", t] = take("sf%d" % t, [P, S])
+            product(2, t, bank["sf", t])
+
+        def sf_copy(t):
+            nc.scalar.copy(out=sf_sb[t][:], in_=bank["sf", t][:])
+
+        def sr_mm(t):
+            bank["sr", t] = take("sr%d" % t, [P, S])
+            product(1, t, bank["sr", t])
+
+        def both_open(t):
+            bank["sr", t] = take("sr%d" % t, [P, S])
+            product(2, t, bank["sr", t], True, False)
+
+        def both_close(t):
+            product(1, t, bank["sr", t], False, True)
+
+        def gather_fr(t, h):
+            nc.scalar.activation(
+                out=nfr[t][:, h * HALF : (h + 1) * HALF],
+                in_=sf_sb[t][:].indirect(reg_sb[:, 16 * h : 16 * (h + 1)]),
+                func=ACT.Copy,
+                scale=-1.0,
+            )
+
+        def turn(source, h, u, first):
+            if first:
+                bank["tt", h, u] = take("tt%d%d" % (h, u), [P, 2, 2, P])
+            for i in range(2):
+                for b in range(2):
+                    c0 = h * HALF + b * P
+                    nc.tensor.matmul(
+                        bank["tt", h, u][:, i, b, :], source[2 * u + i][:, c0 : c0 + P], ident[:],
+                        start=(first and i == 0 and b == 0), stop=(not first and i == 1 and b == 1),
+                        is_transpose=True,
+                    )
+
+        def turn_sf(h, u):
+            turn(sf_sb, h, u, True)
+
+        def turn_fr(h, u):
+            turn(nfr, h, u, False)
+
+        def tanh(h, u):
+            nc.scalar.activation(
+                out=th_t[2 * h + u][:].rearrange("p a b -> p (a b)"),
+                in_=bank["tt", h, u][:].rearrange("p i b c -> p (i b c)"),
+                func=ACT.Tanh,
+                scale=-1.0,
+            )
+
+        def turn_back(h, u):
+            bank["th", h, u] = take("th%d%d" % (h, u), [P, PACK, P])
+            for b in range(PACK):
+                nc.tensor.transpose(bank["th", h, u][:, b, :], th_t[2 * h + u][:, b, :], ident[:])
+
+        def diff(t):
+            nc.vector.tensor_tensor(dif[t][:], bank["sr", t][:], sf_sb[t][:], ALU.add)
+
+        def over_sig(t):
+            nc.vector.tensor_tensor(z[t][:], dif[t][:], inv[t][:], ALU.mult)
+
+        def bank_over_sig(t):
+            nc.vector.tensor_tensor(z[t][:], bank["sr", t][:], inv[t][:], ALU.mult)
+
+        def abs_sum(t):
+            nc.scalar.activation(out=absz[:], in_=z[t][:], func=ACT.Abs, accum_out=sums[t][:])
+
+        def abs_sum_v(t):
+            nc.vector.tensor_reduce(sums[t][:], z[t][:], mybir.AxisListType.X, ALU.add, apply_absolute_value=True)
+
+        def factor(t):
+            nc.vector.tensor_scalar(den[t][:], sums[t][:], 0.2 * S, per_unit[:, t : t + 1], ALU.add, ALU.mult)
+            nc.vector.reciprocal(c1[t][:], den[t][:])
+
+        def unit_factors():
+            nc.vector.tensor_scalar(c2[:], unit_sb[:], 0.6, None, ALU.mult)
+            nc.vector.tensor_scalar(scaled_unit[:], unit_sb[:], -2.0 * S, None, ALU.mult)
+            nc.vector.reciprocal(per_unit[:], scaled_unit[:])
+
+        def grad(t):
+            nc.vector.scalar_tensor_tensor(e[t][:], z[t][:], c1[t][:], sgn[t][:], ALU.mult, ALU.mult)
+
+        def hidden(t, h):
+            nc.vector.scalar_tensor_tensor(
+                hid_p[h][:, t, :],
+                bank["th", h, t // 2][:].rearrange("p b j -> p (b j)")[:, (t % 2) * HALF : (t % 2 + 1) * HALF],
+                c2[:, t : t + 1],
+                e[t][:, h * HALF : (h + 1) * HALF],
+                ALU.mult,
+                ALU.add,
+            )
+
+        def weave(h, eng, c0=0, c1=HALF):
+            dst = hid_i[h][:, c0:c1, :].rearrange("p (c i) t -> p c t i", i=4)
+            src = hid_p[h][:, :, c0:c1].rearrange("p t (c i) -> p c t i", i=4)
+            if eng == "v":
+                nc.vector.tensor_copy(out=dst, in_=src)
+            else:
+                nc.scalar.copy(out=dst, in_=src)
+
+        def quant_h(h):
+            nc.vector.quantize_mx(
+                out=hc[h][:].bitcast(FP8X4), scales=hs[h][:], in_=hid_i[h][:].rearrange("p n j -> p (n j)")
+            )
+
+        def last(h, eng):
+            acc = take("out%d" % h, [P, S])
+            nc.tensor.matmul_mx(
+                out=acc[:, 0:HALF],
+                lhsT=w3c[:].bitcast(FP8X4),
+                lhsT_scale=w3s[:],
+                rhs=hc[h][:].bitcast(FP8X4),
+                rhs_scale=hs[h][:],
+                start=True,
+                stop=True,
+            )
+            if eng == "v":
+                nc.vector.tensor_copy(out=res[h][:], in_=acc[:, 0:HALF])
+            else:
+                nc.scalar.copy(out=res[h][:], in_=acc[:, 0:HALF])
+            nc.sync.dma_start(out=out[:, h * HALF : (h + 1) * HALF], in_=res[h][:])
+
+        inv_root(0)
+        inv_root(1)
+        gather_x()
+        inv_root(2)
+        inv_root(3)
+        inv_square(0)
+        inv_square(1)
+        inv_square(2)
+        inv_square(3)
+        cast_w(2, 0, "v")
+        cast_w(2, 1, "v", 0, 2)
+        cast_w(2, 1, "v", 2, 4)
+        quant_w(2, 0, 2)
+        quant_w(2, 2, 4)
+        sf_mm(0)
+        sf_mm(1)
+        sf_mm(2)
+        sf_mm(3)
+        both_open(0)
+        both_open(1)
+        cast_w(1, 0, "v")
+        sf_copy(0)
+        sf_copy(1)
+        sf_copy(2)
+        sf_copy(3)
+        cast_w(1, 1, "v", 0, 2)
+        cast_w(1, 1, "v", 2, 4)
+        quant_w(1, 0, 2)
+        quant_w(1, 2, 4)
+        both_close(0)
+        both_close(1)
+        sr_mm(2)
+        sr_mm(3)
+        turn_sf(0, 0)
+        turn_sf(0, 1)
+        turn_sf(1, 0)
+        turn_sf(1, 1)
+        bank_over_sig(0)
+        bank_over_sig(1)
+        diff(2)
+        diff(3)
+        over_sig(2)
+        over_sig(3)
+        half_sign(0)
+        half_sign(1)
+        half_sign(2)
+        half_sign(3)
+        unit_factors()
+        gather_fr(0, 0)
+        gather_fr(1, 0)
+        turn_fr(0, 0)
+        gather_fr(2, 0)
+        gather_fr(3, 0)
+        turn_fr(0, 1)
+        abs_sum(0)
+        abs_sum(1)
+        abs_sum_v(2)
+        abs_sum_v(3)
+        factor(2)
+        factor(3)
+        tanh(0, 0)
+        turn_back(0, 0)
+        tanh(0, 1)
+        turn_back(0, 1)
+        grad(2)
+        factor(0)
+        grad(3)
+        factor(1)
+        grad(0)
+        grad(1)
+        cast_w3()
+        gather_fr(0, 1)
+        gather_fr(1, 1)
+        turn_fr(1, 0)
+        hidden(0, 0)
+        hidden(1, 0)
+        quant_w3()
+        gather_fr(2, 1)
+        gather_fr(3, 1)
+        turn_fr(1, 1)
+        hidden(2, 0)
+        hidden(3, 0)
+        tanh(1, 0)
+        turn_back(1, 0)
+        tanh(1, 1)
+        turn_back(1, 1)
+        weave(0, "s")
+        hidden(0, 1)
+        hidden(1, 1)
+        hidden(2, 1)
+        hidden(3, 1)
+        weave(1, "v")
+        quant_h(0)
+        last(0, "s")
+        quant_h(1)
+        last(1, "v")

@@ -36,7 +36,7 @@ def tile_picked_ydmddi_reg_p_kernel(
         reg_sb = sb("reg_sb", [P, S // 16], U16)
         xw = sb("xw", [P, T], I32)
         xs = sb("xs", [P, T], U8)
-        sig_sb = [sb("sig%d" % t, [P, S], F32) for t in range(PACK)]
+        sig_sb = [sb("sig%d" % u, [P, 2, S], F32) for u in range(2)]
         w1_raw = [sb("w1raw%d" % h, [P, PACK, HALF], F32) for h in range(2)]
         w2_raw = [sb("w2raw%d" % h, [P, PACK, HALF], F32) for h in range(2)]
         w3_raw = sb("w3raw", [P, PACK, N], F32)
@@ -53,8 +53,8 @@ def tile_picked_ydmddi_reg_p_kernel(
                 in_=x_scales[0, 4 * q : 4 * q + 4, :].bitcast(I32),
             )
 
-        def load_sig(t):
-            nc.sync.dma_start(out=sig_sb[t][:], in_=sig_v[:, t, :])
+        def load_sig(u):
+            nc.sync.dma_start(out=sig_sb[u][:], in_=sig_v[:, 2 * u : 2 * u + 2, :])
 
         def load_w(raw, view, h):
             nc.sync.dma_start(out=raw[h][:], in_=view[:, :, h * HALF : (h + 1) * HALF])
@@ -66,8 +66,6 @@ def tile_picked_ydmddi_reg_p_kernel(
         nc.sync.dma_start(offs_sb[:], offs)
         load_sig(1)
         load_x()
-        load_sig(2)
-        load_sig(3)
         load_w(w2_raw, w2_v, 0)
         load_w(w2_raw, w2_v, 1)
         nc.sync.dma_start(out=unit_sb[:], in_=unit.rearrange("(p t) o -> p (t o)", t=PACK))
@@ -79,12 +77,17 @@ def tile_picked_ydmddi_reg_p_kernel(
         ident = sb("ident", [P, P], F32)
         make_identity(nc, ident[:])
 
-        root = [sb("root%d" % t, [P, S], F32) for t in range(PACK)]
-        inv = [sb("inv%d" % t, [P, S], F32) for t in range(PACK)]
-        sgn = [sb("sgn%d" % t, [P, S], F32) for t in range(PACK)]
+        root = [sb("root%d" % u, [P, 2, S], F32) for u in range(2)]
+        inv = [sb("inv%d" % u, [P, 2, S], F32) for u in range(2)]
+        sgn = [sb("sgn%d" % u, [P, 2, S], F32) for u in range(2)]
 
         def inv_root(t):
             nc.scalar.activation(out=root[t][:], in_=sig_sb[t][:], func=ACT.Abs_reciprocal_sqrt)
+
+        warm = sb("warm", [P, 1], F32)
+
+        def warm_tanh():
+            nc.scalar.activation(out=warm[:], in_=root[1][:, 1, 0:1], func=ACT.Tanh)
 
         def inv_square(t):
             nc.scalar.activation(out=inv[t][:], in_=root[t][:], func=ACT.Square)
@@ -151,17 +154,17 @@ def tile_picked_ydmddi_reg_p_kernel(
             )
 
         sf_sb = [sb("sf%d" % t, [P, S], F32) for t in range(PACK)]
-        nfr = [sb("nfr%d" % t, [P, S], F32) for t in range(PACK)]
+        nfr = {}
         th_t = [sb("tht%d" % t, [P, PACK, P], F32) for t in range(PACK)]
         dif = [sb("dif%d" % t, [P, S], F32) for t in range(PACK)]
         z = [sb("z%d" % t, [P, S], F32) for t in range(PACK)]
         e = [sb("e%d" % t, [P, S], F32) for t in range(PACK)]
         absz = sb("absz", [P, S], F32)
-        sums = [sb("sum%d" % t, [P, 1], F32) for t in range(PACK)]
-        den = [sb("den%d" % t, [P, 1], F32) for t in range(PACK)]
+        sums = [sb("sum%d" % u, [P, 2], F32) for u in range(2)]
+        den = [sb("den%d" % u, [P, 2], F32) for u in range(2)]
         scaled_unit = sb("scaled_unit", [P, PACK], F32)
         per_unit = sb("per_unit", [P, PACK], F32)
-        c1 = [sb("c1_%d" % t, [P, 1], F32) for t in range(PACK)]
+        c1 = [sb("c1_%d" % u, [P, 2], F32) for u in range(2)]
         c2 = sb("c2", [P, PACK], F32)
         hid_p = [sb("hidp%d" % h, [P, PACK, HALF], BF16) for h in range(2)]
         hid_i = [sb("hidi%d" % h, [P, HALF, PACK], BF16) for h in range(2)]
@@ -169,7 +172,7 @@ def tile_picked_ydmddi_reg_p_kernel(
         hs = [sb("hs%d" % h, [P, HALF], U8) for h in range(2)]
         res = [sb("res%d" % h, [P, HALF], F32) for h in range(2)]
         bank = {}
-        place = {"sf0":0,"sf1":1,"sf2":2,"sf3":3,"sr0":4,"sr1":5,"sr2":6,"sr3":7,"tt00":0,"tt01":1,"tt10":2,"tt11":3,"th00":4,"th01":5,"th10":6,"th11":7,"out0":0,"out1":1}
+        place = {"sf0":0,"sf1":1,"sf2":2,"sf3":3,"sr0":4,"sr1":5,"sr2":6,"sr3":7,"tt00":4,"tt01":5,"tt10":6,"tt11":7,"th00":0,"th01":1,"th10":2,"th11":3,"out0":4,"out1":5}
 
         def take(key, shape):
             tag = "bank%d" % place[key]
@@ -179,8 +182,11 @@ def tile_picked_ydmddi_reg_p_kernel(
             bank["sf", t] = take("sf%d" % t, [P, S])
             product(2, t, bank["sf", t])
 
-        def sf_copy(t):
-            nc.scalar.copy(out=sf_sb[t][:], in_=bank["sf", t][:])
+        def sf_copy(t, eng="s"):
+            if eng == "s":
+                nc.scalar.copy(out=sf_sb[t][:], in_=bank["sf", t][:])
+            else:
+                nc.vector.tensor_copy(out=sf_sb[t][:], in_=bank["sf", t][:])
 
         def sr_mm(t):
             bank["sr", t] = take("sr%d" % t, [P, S])
@@ -194,8 +200,11 @@ def tile_picked_ydmddi_reg_p_kernel(
             product(1, t, bank["sr", t], False, True)
 
         def gather_fr(t, h):
+            if t % 2 == 0:
+                tag = "nfr%d" % (t // 2)
+                nfr[h, t // 2] = keep.tile([P, 2, HALF], F32, name=tag, tag=tag, align_bytes=64)
             nc.scalar.activation(
-                out=nfr[t][:, h * HALF : (h + 1) * HALF],
+                out=nfr[h, t // 2][:, t % 2, :],
                 in_=sf_sb[t][:].indirect(reg_sb[:, 16 * h : 16 * (h + 1)]),
                 func=ACT.Copy,
                 scale=-1.0,
@@ -206,18 +215,17 @@ def tile_picked_ydmddi_reg_p_kernel(
                 bank["tt", h, u] = take("tt%d%d" % (h, u), [P, 2, 2, P])
             for i in range(2):
                 for b in range(2):
-                    c0 = h * HALF + b * P
                     nc.tensor.matmul(
-                        bank["tt", h, u][:, i, b, :], source[2 * u + i][:, c0 : c0 + P], ident[:],
+                        bank["tt", h, u][:, i, b, :], source(i)[:, b * P : (b + 1) * P], ident[:],
                         start=(first and i == 0 and b == 0), stop=(not first and i == 1 and b == 1),
                         is_transpose=True,
                     )
 
         def turn_sf(h, u):
-            turn(sf_sb, h, u, True)
+            turn(lambda i: sf_sb[2 * u + i][:, h * HALF : (h + 1) * HALF], h, u, True)
 
         def turn_fr(h, u):
-            turn(nfr, h, u, False)
+            turn(lambda i: nfr[h, u][:, i, :], h, u, False)
 
         def tanh(h, u):
             nc.scalar.activation(
@@ -235,21 +243,29 @@ def tile_picked_ydmddi_reg_p_kernel(
         def diff(t):
             nc.vector.tensor_tensor(dif[t][:], bank["sr", t][:], sf_sb[t][:], ALU.add)
 
-        def over_sig(t):
-            nc.vector.tensor_tensor(z[t][:], dif[t][:], inv[t][:], ALU.mult)
+        def over_sig(t, eng="v"):
+            (nc.vector if eng == "v" else nc.gpsimd).tensor_tensor(z[t][:], dif[t][:], inv[t // 2][:, t % 2, :], ALU.mult)
 
         def bank_over_sig(t):
-            nc.vector.tensor_tensor(z[t][:], bank["sr", t][:], inv[t][:], ALU.mult)
+            nc.vector.tensor_tensor(z[t][:], bank["sr", t][:], inv[t // 2][:, t % 2, :], ALU.mult)
 
         def abs_sum(t):
-            nc.scalar.activation(out=absz[:], in_=z[t][:], func=ACT.Abs, accum_out=sums[t][:])
+            nc.scalar.activation(out=absz[:], in_=z[t][:], func=ACT.Abs, accum_out=sums[t // 2][:, t % 2 : t % 2 + 1])
 
         def abs_sum_v(t):
-            nc.vector.tensor_reduce(sums[t][:], z[t][:], mybir.AxisListType.X, ALU.add, apply_absolute_value=True)
+            nc.vector.tensor_reduce(sums[t // 2][:, t % 2 : t % 2 + 1], z[t][:], mybir.AxisListType.X, ALU.add, apply_absolute_value=True)
 
-        def factor(t):
-            nc.vector.tensor_scalar(den[t][:], sums[t][:], 0.2 * S, per_unit[:, t : t + 1], ALU.add, ALU.mult)
-            nc.vector.reciprocal(c1[t][:], den[t][:])
+        def divisor(u):
+            nc.vector.scalar_tensor_tensor(
+                den[u][:], sums[u][:], 0.2 * S, per_unit[:, 2 * u : 2 * u + 2], ALU.add, ALU.mult
+            )
+
+        def factor(u):
+            nc.vector.reciprocal(c1[u][:], den[u][:])
+
+        def clock(name, ap):
+            probe = sb(name, [P, 1], F32)
+            nc.gpsimd.tensor_copy(probe[:], ap)
 
         def unit_factors():
             nc.vector.tensor_scalar(c2[:], unit_sb[:], 0.6, None, ALU.mult)
@@ -257,7 +273,7 @@ def tile_picked_ydmddi_reg_p_kernel(
             nc.vector.reciprocal(per_unit[:], scaled_unit[:])
 
         def grad(t):
-            nc.vector.scalar_tensor_tensor(e[t][:], z[t][:], c1[t][:], sgn[t][:], ALU.mult, ALU.mult)
+            nc.vector.scalar_tensor_tensor(e[t][:], z[t][:], c1[t // 2][:, t % 2 : t % 2 + 1], sgn[t // 2][:, t % 2, :], ALU.mult, ALU.mult)
 
         def hidden(t, h):
             nc.vector.scalar_tensor_tensor(
@@ -301,13 +317,10 @@ def tile_picked_ydmddi_reg_p_kernel(
 
         inv_root(0)
         inv_root(1)
+        warm_tanh()
         gather_x()
-        inv_root(2)
-        inv_root(3)
         inv_square(0)
         inv_square(1)
-        inv_square(2)
-        inv_square(3)
         cast_w(2, 0, "v")
         cast_w(2, 1, "v", 0, 2)
         cast_w(2, 1, "v", 2, 4)
@@ -317,8 +330,6 @@ def tile_picked_ydmddi_reg_p_kernel(
         sf_mm(1)
         sf_mm(2)
         sf_mm(3)
-        both_open(0)
-        both_open(1)
         cast_w(1, 0, "v")
         sf_copy(0)
         sf_copy(1)
@@ -328,69 +339,70 @@ def tile_picked_ydmddi_reg_p_kernel(
         cast_w(1, 1, "v", 2, 4)
         quant_w(1, 0, 2)
         quant_w(1, 2, 4)
-        both_close(0)
-        both_close(1)
-        sr_mm(2)
-        sr_mm(3)
-        turn_sf(0, 0)
-        turn_sf(0, 1)
-        turn_sf(1, 0)
-        turn_sf(1, 1)
-        bank_over_sig(0)
-        bank_over_sig(1)
-        diff(2)
-        diff(3)
-        over_sig(2)
-        over_sig(3)
+        sr_mm(0)
+        sr_mm(1)
+        both_open(2)
+        both_close(2)
+        both_open(3)
+        both_close(3)
+        diff(0)
+        diff(1)
+        over_sig(0)
+        over_sig(1)
+        bank_over_sig(2)
+        bank_over_sig(3)
         half_sign(0)
         half_sign(1)
-        half_sign(2)
-        half_sign(3)
         unit_factors()
         gather_fr(0, 0)
         gather_fr(1, 0)
+        turn_sf(0, 0)
         turn_fr(0, 0)
         gather_fr(2, 0)
         gather_fr(3, 0)
+        turn_sf(0, 1)
         turn_fr(0, 1)
         abs_sum(0)
         abs_sum(1)
-        abs_sum_v(2)
-        abs_sum_v(3)
-        factor(2)
-        factor(3)
         tanh(0, 0)
         turn_back(0, 0)
         tanh(0, 1)
         turn_back(0, 1)
-        grad(2)
+        abs_sum_v(2)
+        abs_sum_v(3)
+        cast_w3()
+        divisor(0)
+        divisor(1)
         factor(0)
-        grad(3)
         factor(1)
+        quant_w3()
         grad(0)
         grad(1)
-        cast_w3()
+        grad(2)
+        grad(3)
         gather_fr(0, 1)
         gather_fr(1, 1)
+        turn_sf(1, 0)
         turn_fr(1, 0)
-        hidden(0, 0)
-        hidden(1, 0)
-        quant_w3()
         gather_fr(2, 1)
         gather_fr(3, 1)
+        turn_sf(1, 1)
         turn_fr(1, 1)
-        hidden(2, 0)
-        hidden(3, 0)
         tanh(1, 0)
         turn_back(1, 0)
         tanh(1, 1)
         turn_back(1, 1)
+        hidden(0, 0)
+        hidden(1, 0)
+        hidden(2, 0)
+        hidden(3, 0)
         weave(0, "s")
         hidden(0, 1)
         hidden(1, 1)
         hidden(2, 1)
         hidden(3, 1)
-        weave(1, "v")
+        weave(1, "v", 0, 160)
+        weave(1, "s", 160, 256)
         quant_h(0)
         last(0, "s")
         quant_h(1)

@@ -37,8 +37,8 @@ def tile_picked_ydmddi_reg_p_kernel(
         xw = sb("xw", [P, T], I32)
         xs = sb("xs", [P, T], U8)
         sig_sb = [sb("sig%d" % u, [P, 2, S], F32) for u in range(2)]
-        w1_raw = [sb("w1raw%d" % h, [P, PACK, HALF], F32) for h in range(2)]
-        w2_raw = [sb("w2raw%d" % h, [P, PACK, HALF], F32) for h in range(2)]
+        w1_raw = sb("w1raw", [P, PACK, H], F32)
+        w2_raw = sb("w2raw", [P, PACK, H], F32)
         w3_raw = sb("w3raw", [P, PACK, N], F32)
         unit_sb = sb("unit_sb", [P, PACK], F32)
 
@@ -56,22 +56,24 @@ def tile_picked_ydmddi_reg_p_kernel(
         def load_sig(u):
             nc.sync.dma_start(out=sig_sb[u][:], in_=sig_v[:, 2 * u : 2 * u + 2, :])
 
+        def load_sig_tile(t):
+            nc.sync.dma_start(out=sig_sb[t // 2][:, t % 2, :], in_=sig_v[:, t, :])
+
         def load_w(raw, view, h):
-            nc.sync.dma_start(out=raw[h][:], in_=view[:, :, h * HALF : (h + 1) * HALF])
+            nc.sync.dma_start(out=raw[:], in_=view)
 
         def load_x():
             nc.sync.dma_start(out=xw[:], in_=x_words[0].rearrange("p n t -> p (n t)").bitcast(I32))
 
-        load_sig(0)
+        load_sig_tile(0)
+        load_sig_tile(1)
         nc.sync.dma_start(offs_sb[:], offs)
         load_sig(1)
         load_x()
         load_w(w2_raw, w2_v, 0)
-        load_w(w2_raw, w2_v, 1)
+        load_w(w1_raw, w1_v, 0)
         nc.sync.dma_start(out=unit_sb[:], in_=unit.rearrange("(p t) o -> p (t o)", t=PACK))
         nc.sync.dma_start(reg_sb[:], reg)
-        load_w(w1_raw, w1_v, 0)
-        load_w(w1_raw, w1_v, 1)
         nc.sync.dma_start(out=w3_raw[:], in_=w3.rearrange("(p j) n -> p j n", j=PACK))
 
         ident = sb("ident", [P, P], F32)
@@ -89,11 +91,28 @@ def tile_picked_ydmddi_reg_p_kernel(
         def warm_tanh():
             nc.scalar.activation(out=warm[:], in_=root[1][:, 1, 0:1], func=ACT.Tanh)
 
+        def inv_root_tile(t):
+            nc.scalar.activation(
+                out=root[t // 2][:, t % 2, :], in_=sig_sb[t // 2][:, t % 2, :], func=ACT.Abs_reciprocal_sqrt
+            )
+
         def inv_square(t):
             nc.scalar.activation(out=inv[t][:], in_=root[t][:], func=ACT.Square)
 
         def half_sign(t):
             nc.vector.tensor_scalar(sgn[t][:], sig_sb[t][:], 0.0, 0.5, ALU.is_ge, ALU.subtract)
+
+        signed = sb("signed", [P, 2, S], F32)
+
+        def signed_inv(u):
+            nc.vector.scalar_tensor_tensor(
+                signed[:].rearrange("p t j -> p (t j)"),
+                sgn[u][:].rearrange("p t j -> p (t j)"),
+                2.0,
+                inv[u][:].rearrange("p t j -> p (t j)"),
+                ALU.mult,
+                ALU.mult,
+            )
 
         xg = sb("xg", [P, S], U32)
         xsg = sb("xsg", [P, S], U8)
@@ -108,8 +127,8 @@ def tile_picked_ydmddi_reg_p_kernel(
         wsc = {1: sb("w1s", [P, H], U8), 2: sb("w2s", [P, H], U8)}
 
         def cast_w(w, h, eng, t0=0, t1=PACK):
-            dst = wb[w][:, t0:t1, 64 * h : 64 * (h + 1), :].rearrange("p t m j -> p m j t")
-            src = wraw[w][h][:].rearrange("p j (m t) -> p m j t", t=PACK)[:, :, :, t0:t1]
+            dst = wb[w][:, t0:t1].rearrange("p t m j -> p m j t")
+            src = wraw[w][:].rearrange("p j (m t) -> p m j t", t=PACK)[:, :, :, t0:t1]
             if w == 1 and eng == "v":
                 nc.vector.tensor_scalar(dst, src, -1.0, None, ALU.mult)
             elif w == 1:
@@ -130,7 +149,7 @@ def tile_picked_ydmddi_reg_p_kernel(
         w3c = sb("w3c", [P, N], U32)
         w3s = sb("w3s", [P, N], U8)
 
-        def cast_w3():
+        def cast_w3(eng="v"):
             nc.vector.tensor_copy(
                 out=w3b[:].rearrange("p (c i) j -> p c j i", i=4),
                 in_=w3_raw[:].rearrange("p j (c i) -> p c j i", i=4),
@@ -155,7 +174,6 @@ def tile_picked_ydmddi_reg_p_kernel(
 
         sf_sb = [sb("sf%d" % t, [P, S], F32) for t in range(PACK)]
         nfr = {}
-        th_t = [sb("tht%d" % t, [P, PACK, P], F32) for t in range(PACK)]
         dif = [sb("dif%d" % t, [P, S], F32) for t in range(PACK)]
         z = [sb("z%d" % t, [P, S], F32) for t in range(PACK)]
         e = [sb("e%d" % t, [P, S], F32) for t in range(PACK)]
@@ -172,7 +190,7 @@ def tile_picked_ydmddi_reg_p_kernel(
         hs = [sb("hs%d" % h, [P, HALF], U8) for h in range(2)]
         res = [sb("res%d" % h, [P, HALF], F32) for h in range(2)]
         bank = {}
-        place = {"sf0":0,"sf1":1,"sf2":2,"sf3":3,"sr0":4,"sr1":5,"sr2":6,"sr3":7,"tt00":4,"tt01":5,"tt10":6,"tt11":7,"th00":0,"th01":1,"th10":2,"th11":3,"out0":4,"out1":5}
+        place = {"sf0":0,"sf1":1,"sf2":2,"sf3":3,"sr0":4,"sr1":5,"sr2":6,"sr3":7,"ttA":0,"ttB":1,"ttC":2,"ttD":3,"ttE":0,"thA":4,"thB":5,"thC":6,"thD":7,"thE":1,"out0":2,"out2":3,"out3":0}
 
         def take(key, shape):
             tag = "bank%d" % place[key]
@@ -194,10 +212,14 @@ def tile_picked_ydmddi_reg_p_kernel(
 
         def both_open(t):
             bank["sr", t] = take("sr%d" % t, [P, S])
-            product(2, t, bank["sr", t], True, False)
+            product(1, t, bank["sr", t], True, False)
 
         def both_close(t):
-            product(1, t, bank["sr", t], False, True)
+            product(2, t, bank["sr", t], False, True)
+
+        units = {"A": (0, [0, 1]), "B": (0, [2, 3]), "C": (1, [0, 1]), "D": (1, [2]), "E": (1, [3])}
+        unit_of = {(t, h): k for k, (h, ts) in units.items() for t in ts}
+        th_t = {k: sb("tht" + k, [P, 2 * len(ts), P], F32) for k, (h, ts) in units.items()}
 
         def gather_fr(t, h):
             if t % 2 == 0:
@@ -210,41 +232,38 @@ def tile_picked_ydmddi_reg_p_kernel(
                 scale=-1.0,
             )
 
-        def turn(source, h, u, first):
+        def turn(source, k, first):
+            h, ts = units[k]
             if first:
-                bank["tt", h, u] = take("tt%d%d" % (h, u), [P, 2, 2, P])
-            for i in range(2):
+                bank["tt", k] = take("tt" + k, [P, 2 * len(ts), P])
+            for i, t in enumerate(ts):
                 for b in range(2):
                     nc.tensor.matmul(
-                        bank["tt", h, u][:, i, b, :], source(i)[:, b * P : (b + 1) * P], ident[:],
-                        start=(first and i == 0 and b == 0), stop=(not first and i == 1 and b == 1),
+                        bank["tt", k][:, 2 * i + b, :], source(t, h)[:, b * P : (b + 1) * P], ident[:],
+                        start=(first and i == 0 and b == 0), stop=(not first and t == ts[-1] and b == 1),
                         is_transpose=True,
                     )
 
-        def turn_sf(h, u):
-            turn(lambda i: sf_sb[2 * u + i][:, h * HALF : (h + 1) * HALF], h, u, True)
+        def turn_sf(k):
+            turn(lambda t, h: sf_sb[t][:, h * HALF : (h + 1) * HALF], k, True)
 
-        def turn_fr(h, u):
-            turn(lambda i: nfr[h, u][:, i, :], h, u, False)
+        def turn_fr(k):
+            turn(lambda t, h: nfr[h, t // 2][:, t % 2, :], k, False)
 
-        def tanh(h, u):
-            nc.scalar.activation(
-                out=th_t[2 * h + u][:].rearrange("p a b -> p (a b)"),
-                in_=bank["tt", h, u][:].rearrange("p i b c -> p (i b c)"),
-                func=ACT.Tanh,
-                scale=-1.0,
-            )
+        def tanh(k):
+            nc.scalar.activation(out=th_t[k][:], in_=bank["tt", k][:], func=ACT.Tanh, scale=-1.0)
 
-        def turn_back(h, u):
-            bank["th", h, u] = take("th%d%d" % (h, u), [P, PACK, P])
-            for b in range(PACK):
-                nc.tensor.transpose(bank["th", h, u][:, b, :], th_t[2 * h + u][:, b, :], ident[:])
+        def turn_back(k):
+            blocks = 2 * len(units[k][1])
+            bank["th", k] = take("th" + k, [P, blocks, P])
+            for b in range(blocks):
+                nc.tensor.transpose(bank["th", k][:, b, :], th_t[k][:, b, :], ident[:])
 
         def diff(t):
             nc.vector.tensor_tensor(dif[t][:], bank["sr", t][:], sf_sb[t][:], ALU.add)
 
         def over_sig(t, eng="v"):
-            (nc.vector if eng == "v" else nc.gpsimd).tensor_tensor(z[t][:], dif[t][:], inv[t // 2][:, t % 2, :], ALU.mult)
+            (nc.vector if eng == "v" else nc.gpsimd).tensor_tensor(z[t][:], dif[t][:], signed[:, t, :], ALU.mult)
 
         def bank_over_sig(t):
             nc.vector.tensor_tensor(z[t][:], bank["sr", t][:], inv[t // 2][:, t % 2, :], ALU.mult)
@@ -269,16 +288,21 @@ def tile_picked_ydmddi_reg_p_kernel(
 
         def unit_factors():
             nc.vector.tensor_scalar(c2[:], unit_sb[:], 0.6, None, ALU.mult)
-            nc.vector.tensor_scalar(scaled_unit[:], unit_sb[:], -2.0 * S, None, ALU.mult)
+            nc.vector.tensor_scalar(scaled_unit[:, 0:2], unit_sb[:, 0:2], -1.0 * S, None, ALU.mult)
+            nc.vector.tensor_scalar(scaled_unit[:, 2:4], unit_sb[:, 2:4], -2.0 * S, None, ALU.mult)
             nc.vector.reciprocal(per_unit[:], scaled_unit[:])
 
         def grad(t):
             nc.vector.scalar_tensor_tensor(e[t][:], z[t][:], c1[t // 2][:, t % 2 : t % 2 + 1], sgn[t // 2][:, t % 2, :], ALU.mult, ALU.mult)
 
+        def grad_q(t, eng):
+            nc.vector.tensor_scalar(e[t][:], z[t][:], c1[0][:, t : t + 1], None, ALU.mult)
+
         def hidden(t, h):
+            i = units[unit_of[t, h]][1].index(t)
             nc.vector.scalar_tensor_tensor(
                 hid_p[h][:, t, :],
-                bank["th", h, t // 2][:].rearrange("p b j -> p (b j)")[:, (t % 2) * HALF : (t % 2 + 1) * HALF],
+                bank["th", unit_of[t, h]][:, 2 * i : 2 * i + 2, :].rearrange("p b j -> p (b j)"),
                 c2[:, t : t + 1],
                 e[t][:, h * HALF : (h + 1) * HALF],
                 ALU.mult,
@@ -293,51 +317,57 @@ def tile_picked_ydmddi_reg_p_kernel(
             else:
                 nc.scalar.copy(out=dst, in_=src)
 
-        def quant_h(h):
+        def quant_h(h, c0=0, c1=HALF):
             nc.vector.quantize_mx(
-                out=hc[h][:].bitcast(FP8X4), scales=hs[h][:], in_=hid_i[h][:].rearrange("p n j -> p (n j)")
+                out=hc[h][:, c0:c1].bitcast(FP8X4),
+                scales=hs[h][:, c0:c1],
+                in_=hid_i[h][:, c0:c1, :].rearrange("p n j -> p (n j)"),
             )
 
-        def last(h, eng):
-            acc = take("out%d" % h, [P, S])
+        def last(key, h, eng, c0=0, c1=HALF):
+            acc = take(key, [P, c1 - c0])
             nc.tensor.matmul_mx(
-                out=acc[:, 0:HALF],
+                out=acc[:],
                 lhsT=w3c[:].bitcast(FP8X4),
                 lhsT_scale=w3s[:],
-                rhs=hc[h][:].bitcast(FP8X4),
-                rhs_scale=hs[h][:],
+                rhs=hc[h][:, c0:c1].bitcast(FP8X4),
+                rhs_scale=hs[h][:, c0:c1],
                 start=True,
                 stop=True,
             )
             if eng == "v":
-                nc.vector.tensor_copy(out=res[h][:], in_=acc[:, 0:HALF])
+                nc.vector.tensor_copy(out=res[h][:, c0:c1], in_=acc[:])
             else:
-                nc.scalar.copy(out=res[h][:], in_=acc[:, 0:HALF])
-            nc.sync.dma_start(out=out[:, h * HALF : (h + 1) * HALF], in_=res[h][:])
+                nc.scalar.copy(out=res[h][:, c0:c1], in_=acc[:])
 
-        inv_root(0)
+        def store(h, c0=0, c1=HALF):
+            nc.sync.dma_start(out=out[:, h * HALF + c0 : h * HALF + c1], in_=res[h][:, c0:c1])
+
+        inv_root_tile(0)
+        inv_root_tile(1)
+        inv_square(0)
         inv_root(1)
         warm_tanh()
         gather_x()
-        inv_square(0)
-        inv_square(1)
-        cast_w(2, 0, "v")
-        cast_w(2, 1, "v", 0, 2)
-        cast_w(2, 1, "v", 2, 4)
+        half_sign(0)
+        half_sign(1)
+        signed_inv(0)
+        cast_w(2, 0, "v", 0, 2)
+        cast_w(2, 0, "s", 2, 4)
         quant_w(2, 0, 2)
         quant_w(2, 2, 4)
+        inv_square(1)
         sf_mm(0)
         sf_mm(1)
         sf_mm(2)
         sf_mm(3)
-        cast_w(1, 0, "v")
         sf_copy(0)
         sf_copy(1)
         sf_copy(2)
         sf_copy(3)
-        cast_w(1, 1, "v", 0, 2)
-        cast_w(1, 1, "v", 2, 4)
+        cast_w(1, 0, "v", 0, 2)
         quant_w(1, 0, 2)
+        cast_w(1, 0, "v", 2, 4)
         quant_w(1, 2, 4)
         sr_mm(0)
         sr_mm(1)
@@ -345,53 +375,55 @@ def tile_picked_ydmddi_reg_p_kernel(
         both_close(2)
         both_open(3)
         both_close(3)
+        unit_factors()
         diff(0)
         diff(1)
-        over_sig(0)
-        over_sig(1)
+        over_sig(0, "g")
+        over_sig(1, "g")
         bank_over_sig(2)
         bank_over_sig(3)
-        half_sign(0)
-        half_sign(1)
-        unit_factors()
         gather_fr(0, 0)
         gather_fr(1, 0)
-        turn_sf(0, 0)
-        turn_fr(0, 0)
+        turn_sf("A")
+        turn_fr("A")
         gather_fr(2, 0)
         gather_fr(3, 0)
-        turn_sf(0, 1)
-        turn_fr(0, 1)
-        abs_sum(0)
-        abs_sum(1)
-        tanh(0, 0)
-        turn_back(0, 0)
-        tanh(0, 1)
-        turn_back(0, 1)
-        abs_sum_v(2)
+        turn_sf("B")
+        turn_fr("B")
+        abs_sum(2)
+        tanh("A")
+        turn_back("A")
+        tanh("B")
+        turn_back("B")
         abs_sum_v(3)
-        cast_w3()
-        divisor(0)
+        abs_sum_v(0)
+        abs_sum_v(1)
         divisor(1)
-        factor(0)
+        divisor(0)
         factor(1)
-        quant_w3()
-        grad(0)
-        grad(1)
+        factor(0)
         grad(2)
         grad(3)
+        grad_q(0, "v")
+        grad_q(1, "v")
+        cast_w3("v")
+        quant_w3()
         gather_fr(0, 1)
         gather_fr(1, 1)
-        turn_sf(1, 0)
-        turn_fr(1, 0)
+        turn_sf("C")
+        turn_fr("C")
         gather_fr(2, 1)
+        turn_sf("D")
+        turn_fr("D")
         gather_fr(3, 1)
-        turn_sf(1, 1)
-        turn_fr(1, 1)
-        tanh(1, 0)
-        turn_back(1, 0)
-        tanh(1, 1)
-        turn_back(1, 1)
+        turn_sf("E")
+        turn_fr("E")
+        tanh("C")
+        turn_back("C")
+        tanh("D")
+        turn_back("D")
+        tanh("E")
+        turn_back("E")
         hidden(0, 0)
         hidden(1, 0)
         hidden(2, 0)
@@ -401,9 +433,13 @@ def tile_picked_ydmddi_reg_p_kernel(
         hidden(1, 1)
         hidden(2, 1)
         hidden(3, 1)
-        weave(1, "v", 0, 160)
-        weave(1, "s", 160, 256)
         quant_h(0)
-        last(0, "s")
-        quant_h(1)
-        last(1, "v")
+        weave(1, "v", 0, 128)
+        weave(1, "s", 128, 256)
+        last("out0", 0, "s")
+        store(0)
+        quant_h(1, 0, 128)
+        quant_h(1, 128, 256)
+        last("out2", 1, "s", 0, 128)
+        last("out3", 1, "v", 128, 256)
+        store(1)

from contextlib import ExitStack

import concourse.mybir as mybir
from concourse.masks import make_identity

K, T, S, N, H = 512, 1024, 512, 128, 512
FLOPS = 2 * K * H * S * 2 + 2 * H * N * S

F32 = mybir.dt.float32
BF16 = mybir.dt.bfloat16
I32 = mybir.dt.int32
U32 = mybir.dt.uint32
U16 = mybir.dt.uint16
U8 = mybir.dt.uint8
FP8X4 = mybir.dt.float8_e4m3fn_x4
ALU = mybir.AluOpType
ACT = mybir.ActivationFunctionType

P = 128
PACK = 4
HALF = 256


def tile_picked_ydmddi_reg_p_kernel(
    tc, x_words, x_scales, w1, w2, sig, unit, w3, offs, reg, out
):
    nc = tc.nc
    with ExitStack() as ctx:
        keep = ctx.enter_context(tc.tile_pool(name="keep", bufs=1))
        psum = ctx.enter_context(tc.psum_pool(name="psum", bufs=1))

        def sb(name, shape, dtype):
            return keep.tile(shape, dtype, name=name, align_bytes=64)

        offs_sb = sb("offs_sb", [P, S // 16], U16)
        reg_sb = sb("reg_sb", [P, S // 16], U16)
        xw = sb("xw", [P, T], I32)
        xs = sb("xs", [P, T], U8)
        sig_sb = [sb("sig%d" % u, [P, 2, S], F32) for u in range(2)]
        w1_raw = sb("w1raw", [P, PACK, H], F32)
        w2_raw = sb("w2raw", [P, PACK, H], F32)
        w3_raw = sb("w3raw", [P, PACK, N], F32)
        unit_sb = sb("unit_sb", [P, PACK], F32)

        sig_v = sig.rearrange("(p t) j -> p t j", t=PACK)
        w1_v = w1.rearrange("(p j) c -> p j c", j=PACK)
        w2_v = w2.rearrange("(p j) c -> p j c", j=PACK)

        nc.vector.memset(xs[:].bitcast(I32), 0)
        for q in range(4):
            nc.scalar.dma_start(
                out=xs[32 * q : 32 * q + 4, :].bitcast(I32),
                in_=x_scales[0, 4 * q : 4 * q + 4, :].bitcast(I32),
            )

        def load_sig(u):
            nc.sync.dma_start(out=sig_sb[u][:], in_=sig_v[:, 2 * u : 2 * u + 2, :])

        def load_sig_tile(t):
            nc.sync.dma_start(out=sig_sb[t // 2][:, t % 2, :], in_=sig_v[:, t, :])

        def load_w(raw, view, h):
            nc.sync.dma_start(out=raw[:], in_=view)

        def load_x():
            nc.sync.dma_start(out=xw[:], in_=x_words[0].rearrange("p n t -> p (n t)").bitcast(I32))

        load_sig_tile(0)
        load_sig_tile(1)
        nc.sync.dma_start(offs_sb[:], offs)
        load_sig(1)
        load_x()
        load_w(w2_raw, w2_v, 0)
        load_w(w1_raw, w1_v, 0)
        nc.sync.dma_start(out=unit_sb[:], in_=unit.rearrange("(p t) o -> p (t o)", t=PACK))
        nc.sync.dma_start(reg_sb[:], reg)
        nc.sync.dma_start(out=w3_raw[:], in_=w3.rearrange("(p j) n -> p j n", j=PACK))

        ident = sb("ident", [P, P], F32)
        make_identity(nc, ident[:])

        root = [sb("root%d" % u, [P, 2, S], F32) for u in range(2)]
        inv = [sb("inv%d" % u, [P, 2, S], F32) for u in range(2)]
        sgn = [sb("sgn%d" % u, [P, 2, S], F32) for u in range(2)]

        def inv_root(t):
            nc.scalar.activation(out=root[t][:], in_=sig_sb[t][:], func=ACT.Abs_reciprocal_sqrt)

        warm = sb("warm", [P, 1], F32)

        def warm_tanh():
            nc.scalar.activation(out=warm[:], in_=root[1][:, 1, 0:1], func=ACT.Tanh)

        def inv_root_tile(t):
            nc.scalar.activation(
                out=root[t // 2][:, t % 2, :], in_=sig_sb[t // 2][:, t % 2, :], func=ACT.Abs_reciprocal_sqrt
            )

        def inv_square(t):
            nc.scalar.activation(out=inv[t][:], in_=root[t][:], func=ACT.Square)

        def half_sign(t):
            nc.vector.tensor_scalar(sgn[t][:], sig_sb[t][:], 0.0, 0.5, ALU.is_ge, ALU.subtract)

        signed = sb("signed", [P, 2, S], F32)

        def signed_inv(u):
            nc.vector.scalar_tensor_tensor(
                signed[:].rearrange("p t j -> p (t j)"),
                sgn[u][:].rearrange("p t j -> p (t j)"),
                2.0,
                inv[u][:].rearrange("p t j -> p (t j)"),
                ALU.mult,
                ALU.mult,
            )

        xg = sb("xg", [P, S], U32)
        xsg = sb("xsg", [P, S], U8)

        def gather_x():
            nc.vector.tensor_copy(xg[:], xw[:].bitcast(U32).indirect(offs_sb[:]))
            nc.vector.tensor_copy(xsg[:], xs[:].indirect(offs_sb[:]))

        wb = {1: sb("w1b", [P, PACK, P, PACK], BF16), 2: sb("w2b", [P, PACK, P, PACK], BF16)}
        wraw = {1: w1_raw, 2: w2_raw}
        wc = {1: sb("w1c", [P, H], U32), 2: sb("w2c", [P, H], U32)}
        wsc = {1: sb("w1s", [P, H], U8), 2: sb("w2s", [P, H], U8)}

        def cast_w(w, h, eng, t0=0, t1=PACK):
            dst = wb[w][:, t0:t1].rearrange("p t m j -> p m j t")
            src = wraw[w][:].rearrange("p j (m t) -> p m j t", t=PACK)[:, :, :, t0:t1]
            if w == 1 and eng == "v":
                nc.vector.tensor_scalar(dst, src, -1.0, None, ALU.mult)
            elif w == 1:
                nc.scalar.activation(out=dst, in_=src, func=ACT.Copy, scale=-1.0)
            elif eng == "v":
                nc.vector.tensor_copy(out=dst, in_=src)
            else:
                nc.scalar.copy(out=dst, in_=src)

        def quant_w(w, t0, t1):
            nc.vector.quantize_mx(
                out=wc[w][:, t0 * P : t1 * P].bitcast(FP8X4),
                scales=wsc[w][:, t0 * P : t1 * P],
                in_=wb[w][:, t0:t1].rearrange("p t m j -> p (t m j)"),
            )

        w3b = sb("w3b", [P, N, PACK], BF16)
        w3c = sb("w3c", [P, N], U32)
        w3s = sb("w3s", [P, N], U8)

        def cast_w3(eng="v"):
            nc.vector.tensor_copy(
                out=w3b[:].rearrange("p (c i) j -> p c j i", i=4),
                in_=w3_raw[:].rearrange("p j (c i) -> p c j i", i=4),
            )

        def quant_w3():
            nc.vector.quantize_mx(
                out=w3c[:].bitcast(FP8X4), scales=w3s[:], in_=w3b[:].rearrange("p n j -> p (n j)")
            )

        def product(w, t, bank, start=True, stop=True):
            cols = slice(t * P, (t + 1) * P)
            nc.tensor.matmul_mx(
                out=bank[:],
                lhsT=wc[w][:, cols].bitcast(FP8X4),
                lhsT_scale=wsc[w][:, cols],
                rhs=xg[:].bitcast(FP8X4),
                rhs_scale=xsg[:],
                start=start,
                stop=stop,
            )

        sf_sb = [sb("sf%d" % t, [P, S], F32) for t in range(PACK)]
        nfr = {}
        dif = [sb("dif%d" % t, [P, S], F32) for t in range(PACK)]
        z = [sb("z%d" % t, [P, S], F32) for t in range(PACK)]
        e = [sb("e%d" % t, [P, S], F32) for t in range(PACK)]
        absz = sb("absz", [P, S], F32)
        sums = [sb("sum%d" % u, [P, 2], F32) for u in range(2)]
        den = [sb("den%d" % u, [P, 2], F32) for u in range(2)]
        scaled_unit = sb("scaled_unit", [P, PACK], F32)
        per_unit = sb("per_unit", [P, PACK], F32)
        c1 = [sb("c1_%d" % u, [P, 2], F32) for u in range(2)]
        c2 = sb("c2", [P, PACK], F32)
        hid_p = [sb("hidp%d" % h, [P, PACK, HALF], BF16) for h in range(2)]
        hid_i = [sb("hidi%d" % h, [P, HALF, PACK], BF16) for h in range(2)]
        hc = [sb("hc%d" % h, [P, HALF], U32) for h in range(2)]
        hs = [sb("hs%d" % h, [P, HALF], U8) for h in range(2)]
        res = [sb("res%d" % h, [P, HALF], F32) for h in range(2)]
        bank = {}
        place = {"sf0":0,"sf1":1,"sf2":2,"sf3":3,"sr0":4,"sr1":5,"sr2":6,"sr3":7,"ttA":0,"ttB":1,"ttC":2,"ttD":3,"ttE":0,"thA":4,"thB":5,"thC":6,"thD":7,"thE":1,"out0":2,"out2":3,"out3":0}

        def take(key, shape):
            tag = "bank%d" % place[key]
            return psum.tile(shape, F32, name=tag, tag=tag, bufs=1)

        def sf_mm(t):
            bank["sf", t] = take("sf%d" % t, [P, S])
            product(2, t, bank["sf", t])

        def sf_copy(t, eng="s"):
            if eng == "s":
                nc.scalar.copy(out=sf_sb[t][:], in_=bank["sf", t][:])
            else:
                nc.vector.tensor_copy(out=sf_sb[t][:], in_=bank["sf", t][:])

        def sr_mm(t):
            bank["sr", t] = take("sr%d" % t, [P, S])
            product(1, t, bank["sr", t])

        def both_open(t):
            bank["sr", t] = take("sr%d" % t, [P, S])
            product(1, t, bank["sr", t], True, False)

        def both_close(t):
            product(2, t, bank["sr", t], False, True)

        units = {"A": (0, [0, 1]), "B": (0, [2, 3]), "C": (1, [0, 1]), "D": (1, [2]), "E": (1, [3])}
        unit_of = {(t, h): k for k, (h, ts) in units.items() for t in ts}
        th_t = {k: sb("tht" + k, [P, 2 * len(ts), P], F32) for k, (h, ts) in units.items()}

        def gather_fr(t, h):
            if t % 2 == 0:
                tag = "nfr%d" % (t // 2)
                nfr[h, t // 2] = keep.tile([P, 2, HALF], F32, name=tag, tag=tag, align_bytes=64)
            nc.scalar.activation(
                out=nfr[h, t // 2][:, t % 2, :],
                in_=sf_sb[t][:].indirect(reg_sb[:, 16 * h : 16 * (h + 1)]),
                func=ACT.Copy,
                scale=-1.0,
            )

        def turn(source, k, first):
            h, ts = units[k]
            if first:
                bank["tt", k] = take("tt" + k, [P, 2 * len(ts), P])
            for i, t in enumerate(ts):
                for b in range(2):
                    nc.tensor.matmul(
                        bank["tt", k][:, 2 * i + b, :], source(t, h)[:, b * P : (b + 1) * P], ident[:],
                        start=(first and i == 0 and b == 0), stop=(not first and t == ts[-1] and b == 1),
                        is_transpose=True,
                    )

        def turn_sf(k):
            turn(lambda t, h: sf_sb[t][:, h * HALF : (h + 1) * HALF], k, True)

        def turn_fr(k):
            turn(lambda t, h: nfr[h, t // 2][:, t % 2, :], k, False)

        def tanh(k):
            nc.scalar.activation(out=th_t[k][:], in_=bank["tt", k][:], func=ACT.Tanh, scale=-1.0)

        def turn_back(k):
            blocks = 2 * len(units[k][1])
            bank["th", k] = take("th" + k, [P, blocks, P])
            for b in range(blocks):
                nc.tensor.transpose(bank["th", k][:, b, :], th_t[k][:, b, :], ident[:])

        def diff(t):
            nc.vector.tensor_tensor(dif[t][:], bank["sr", t][:], sf_sb[t][:], ALU.add)

        def over_sig(t, eng="v"):
            (nc.vector if eng == "v" else nc.gpsimd).tensor_tensor(z[t][:], dif[t][:], signed[:, t, :], ALU.mult)

        def bank_over_sig(t):
            nc.vector.tensor_tensor(z[t][:], bank["sr", t][:], inv[t // 2][:, t % 2, :], ALU.mult)

        def abs_sum(t):
            nc.scalar.activation(out=absz[:], in_=z[t][:], func=ACT.Abs, accum_out=sums[t // 2][:, t % 2 : t % 2 + 1])

        def abs_sum_v(t):
            nc.vector.tensor_reduce(sums[t // 2][:, t % 2 : t % 2 + 1], z[t][:], mybir.AxisListType.X, ALU.add, apply_absolute_value=True)

        def divisor(u):
            nc.vector.scalar_tensor_tensor(
                den[u][:], sums[u][:], 0.2 * S, per_unit[:, 2 * u : 2 * u + 2], ALU.add, ALU.mult
            )

        def factor(u):
            nc.vector.reciprocal(c1[u][:], den[u][:])

        def clock(name, ap):
            probe = sb(name, [P, 1], F32)
            nc.gpsimd.tensor_copy(probe[:], ap)

        def unit_factors():
            nc.vector.tensor_scalar(c2[:], unit_sb[:], 0.6, None, ALU.mult)
            nc.vector.tensor_scalar(scaled_unit[:, 0:2], unit_sb[:, 0:2], -1.0 * S, None, ALU.mult)
            nc.vector.tensor_scalar(scaled_unit[:, 2:4], unit_sb[:, 2:4], -2.0 * S, None, ALU.mult)
            nc.vector.reciprocal(per_unit[:], scaled_unit[:])

        def grad(t):
            nc.vector.scalar_tensor_tensor(e[t][:], z[t][:], c1[t // 2][:, t % 2 : t % 2 + 1], sgn[t // 2][:, t % 2, :], ALU.mult, ALU.mult)

        def grad_q(t, eng):
            nc.vector.tensor_scalar(e[t][:], z[t][:], c1[0][:, t : t + 1], None, ALU.mult)

        def hidden(t, h):
            i = units[unit_of[t, h]][1].index(t)
            nc.vector.scalar_tensor_tensor(
                hid_p[h][:, t, :],
                bank["th", unit_of[t, h]][:, 2 * i : 2 * i + 2, :].rearrange("p b j -> p (b j)"),
                c2[:, t : t + 1],
                e[t][:, h * HALF : (h + 1) * HALF],
                ALU.mult,
                ALU.add,
            )

        def weave(h, eng, c0=0, c1=HALF):
            dst = hid_i[h][:, c0:c1, :].rearrange("p (c i) t -> p c t i", i=4)
            src = hid_p[h][:, :, c0:c1].rearrange("p t (c i) -> p c t i", i=4)
            if eng == "v":
                nc.vector.tensor_copy(out=dst, in_=src)
            else:
                nc.scalar.copy(out=dst, in_=src)

        def quant_h(h, c0=0, c1=HALF):
            nc.vector.quantize_mx(
                out=hc[h][:, c0:c1].bitcast(FP8X4),
                scales=hs[h][:, c0:c1],
                in_=hid_i[h][:, c0:c1, :].rearrange("p n j -> p (n j)"),
            )

        def last(key, h, eng, c0=0, c1=HALF):
            acc = take(key, [P, c1 - c0])
            nc.tensor.matmul_mx(
                out=acc[:],
                lhsT=w3c[:].bitcast(FP8X4),
                lhsT_scale=w3s[:],
                rhs=hc[h][:, c0:c1].bitcast(FP8X4),
                rhs_scale=hs[h][:, c0:c1],
                start=True,
                stop=True,
            )
            if eng == "v":
                nc.vector.tensor_copy(out=res[h][:, c0:c1], in_=acc[:])
            else:
                nc.scalar.copy(out=res[h][:, c0:c1], in_=acc[:])

        def store(h, c0=0, c1=HALF):
            nc.sync.dma_start(out=out[:, h * HALF + c0 : h * HALF + c1], in_=res[h][:, c0:c1])

        inv_root_tile(0)
        inv_root_tile(1)
        inv_square(0)
        inv_root(1)
        warm_tanh()
        gather_x()
        half_sign(0)
        half_sign(1)
        signed_inv(0)
        cast_w(2, 0, "v", 0, 2)
        cast_w(2, 0, "s", 2, 4)
        quant_w(2, 0, 2)
        quant_w(2, 2, 4)
        inv_square(1)
        sf_mm(0)
        sf_mm(1)
        sf_mm(2)
        sf_mm(3)
        sf_copy(0)
        sf_copy(1)
        sf_copy(2)
        sf_copy(3)
        cast_w(1, 0, "v", 0, 2)
        quant_w(1, 0, 2)
        cast_w(1, 0, "v", 2, 4)
        quant_w(1, 2, 4)
        sr_mm(0)
        sr_mm(1)
        both_open(2)
        both_close(2)
        both_open(3)
        both_close(3)
        unit_factors()
        diff(0)
        diff(1)
        over_sig(0, "g")
        over_sig(1, "g")
        bank_over_sig(2)
        bank_over_sig(3)
        gather_fr(0, 0)
        gather_fr(1, 0)
        turn_sf("A")
        turn_fr("A")
        gather_fr(2, 0)
        gather_fr(3, 0)
        turn_sf("B")
        turn_fr("B")
        abs_sum(2)
        tanh("A")
        turn_back("A")
        tanh("B")
        turn_back("B")
        abs_sum_v(3)
        abs_sum_v(0)
        abs_sum_v(1)
        divisor(1)
        divisor(0)
        factor(1)
        factor(0)
        grad(2)
        grad(3)
        grad_q(0, "v")
        grad_q(1, "v")
        cast_w3("v")
        quant_w3()
        gather_fr(0, 1)
        gather_fr(1, 1)
        turn_sf("C")
        turn_fr("C")
        gather_fr(2, 1)
        turn_sf("D")
        turn_fr("D")
        gather_fr(3, 1)
        turn_sf("E")
        turn_fr("E")
        tanh("C")
        turn_back("C")
        tanh("D")
        turn_back("D")
        tanh("E")
        turn_back("E")
        hidden(0, 0)
        hidden(1, 0)
        hidden(2, 0)
        hidden(3, 0)
        weave(0, "s")
        hidden(0, 1)
        hidden(1, 1)
        hidden(2, 1)
        hidden(3, 1)
        quant_h(0)
        weave(1, "v", 0, 128)
        weave(1, "s", 128, 256)
        last("out0", 0, "s")
        store(0)
        quant_h(1, 0, 128)
        quant_h(1, 128, 256)
        last("out2", 1, "s", 0, 128)
        last("out3", 1, "v", 128, 256)
        store(1)
